import numpy as np
import ml_dtypes


def mxq(x, axis, fmt="e4m3"):
    dtype, down = {"e4m3": (ml_dtypes.float8_e4m3fn, 7), "e5m2": (ml_dtypes.float8_e5m2, 14)}[fmt]
    v = np.moveaxis(np.asarray(x, np.float32).astype(ml_dtypes.bfloat16).astype(np.float64), axis, -1)
    blocks = v.reshape(v.shape[:-1] + (-1, 32))
    amax = np.abs(blocks).max(-1, keepdims=True)
    byte = np.maximum(np.where(amax > 0, np.frexp(amax)[1] - 1 + 127, 0) - down, 1)
    scale = np.exp2(byte - 127.0)
    codes = (blocks / scale).astype(np.float32).astype(dtype).astype(np.float64)
    return np.moveaxis((codes * scale).reshape(v.shape), -1, axis)


WIDE = False


def mx_kscale(k):
    if not WIDE:
        return np.ones(k)
    levels = np.array([10, -10, 5, -5, 0])
    if k % 512:
        return np.exp2(np.random.permutation(np.resize(levels, k // 32))).repeat(32)
    a = np.empty((k // 512, 16))
    for p in range(k // 512):
        a[p, :8] = np.random.permutation(np.resize(levels, 8))
        for g in range(8):
            far = levels[np.abs(levels - a[p, g]) >= 10]
            a[p, g + 8] = far[np.random.randint(len(far))]
    return np.exp2(a.ravel()).repeat(32)


def f64(x):
    return np.asarray(x).astype(np.float64)


def striped(idx):
    return np.tile(idx.reshape(-1, 16).T, (8, 1)).astype(np.uint16)


def unstriped(offs):
    return offs[:16].T.reshape(-1).astype(np.int64)


def striped8(idx):
    return np.concatenate([x.reshape(-1, 16).T for x in idx]).astype(np.uint16)


def runs(offs, k):
    lists = np.stack([offs[16 * r : 16 * r + 16].T.reshape(-1) for r in range(8)]).astype(np.int64)
    return lists[np.arange(k) % 512 // 64]


def pack_weight(w):
    k, n = w.shape
    w = f64(np.asarray(w, np.float32).astype(ml_dtypes.bfloat16)).reshape(k // 32, 32, n)
    amax = np.abs(w).max(1)
    byte = np.clip(np.where(amax > 0, np.frexp(amax)[1] - 1 + 127 - 7, 1), 1, 254)
    scaled = (w * np.exp2(127.0 - byte)[:, None, :]).reshape(k, n).astype(np.float32)
    words = np.ascontiguousarray(scaled.reshape(k // 512, 128, 4, n).transpose(0, 1, 3, 2)).astype(ml_dtypes.float8_e4m3fn).view(np.uint8)
    return words, np.ascontiguousarray(byte.astype(np.uint8).reshape(k // 512, 16, n))


def unpack_weight(words, scales):
    g, p, n, _ = words.shape
    vals = np.ascontiguousarray(words).view(ml_dtypes.float8_e4m3fn).astype(np.float64) * np.repeat(np.exp2(scales.astype(np.float64) - 127.0), 8, axis=1)[..., None]
    return vals.transpose(0, 1, 3, 2).reshape(g * 512, n)


def relu(v):
    return np.maximum(v, 0.0)


K, T, S, H, U, C, W = 512, 2048, 512, 512, 1024, 512, 4096


def setup_inputs():
    n = np.random.standard_normal
    s = mx_kscale(K)[:, None]
    packed_xT = pack_weight(n((K, T)) * s)
    return {
        "x_words": packed_xT[0],
        "x_scales": packed_xT[1],
        "w1": (n((K, H)) / np.sqrt(K) / s).astype(np.float32),
        "gs": (np.random.uniform(0.5, 1.5, (K, 1)) / s).astype(np.float32),
        "offs": striped8(np.random.randint(0, T, (8, S))),
        "n1": striped8(np.stack([np.random.permutation(U)[:S] for _ in range(8)])),
        "n2": striped8(np.stack([np.random.permutation(S) for _ in range(8)])),
        "cand": striped8(np.random.randint(0, T, (8, C))),
        "n3": striped(np.random.randint(0, U, W)),
    }


def reference(x_words, x_scales, w1, gs, offs, n1, n2, cand, n3):
    x_cand = unpack_weight(x_words, x_scales)[np.arange(K)[:, None], runs(cand, K)]
    xq = unpack_weight(x_words, x_scales)[np.arange(K)[:, None], runs(offs, K)]
    y = mxq(f64(w1), 0, "e4m3").T @ xq
    nw = y - (relu(y[np.arange(H)[:, None], runs(n2, H)]))
    pg = np.zeros((H, U))
    pg[np.arange(H)[:, None], runs(n1, H)] = nw
    z = f64(gs) * pg
    s = 0.0625 * ((x_cand.T @ mxq(z, 0, "e4m3")))
    mb = s[:, unstriped(n3)]
    mx = mb.reshape(C, U, 4).max(axis=2)
    mn = mb.reshape(C, U, 4).min(axis=2)
    return mx - (0.5 * mn)

@@ -1,0 +1,171 @@
+from contextlib import ExitStack
+
+import concourse.mybir as mybir
+
+F32 = mybir.dt.float32
+BF16 = mybir.dt.bfloat16
+I32 = mybir.dt.int32
+U32 = mybir.dt.uint32
+U16 = mybir.dt.uint16
+U8 = mybir.dt.uint8
+FP8X4 = mybir.dt.float8_e4m3fn_x4
+ALU = mybir.AluOpType
+ACT = mybir.ActivationFunctionType
+
+P = 128
+PACK = 4
+K, T, S, H, U, C, W = 512, 2048, 512, 512, 1024, 512, 4096
+MEMBERS = 4
+STRIPE = 16
+BANK = 512
+SPARE = 32
+PIECE = 1024
+Z_SCALAR_COLS = 384
+
+FLOPS = 2 * K * H * S + 2 * K * C * U
+
+
+def tile_picked_hcandpagezgspan_none_p_kernel(tc, x_words, x_scales, w1, gs, offs, n1, n2, cand, n3, out):
+    nc = tc.nc
+    with ExitStack() as ctx:
+        lists = ctx.enter_context(tc.tile_pool(name="lists", bufs=1))
+        keep = ctx.enter_context(tc.tile_pool(name="keep", bufs=1))
+        ring = ctx.enter_context(tc.tile_pool(name="ring", bufs=2))
+        psum = ctx.enter_context(tc.psum_pool(name="psum", bufs=8))
+
+        def load_list(src, name):
+            tile = lists.tile(list(src.shape), U16, name=name)
+            nc.sync.dma_start(tile[:], src)
+            return tile
+
+        table_scales = keep.tile([P, T], U8, name="table_scales")
+        rows = x_scales[0].bitcast(I32)
+        nc.sync.dma_start(table_scales[:].bitcast(I32), rows.unsqueeze(1).to_broadcast([16, 8, T // 4]))
+        offs_sb = load_list(offs, "offs_sb")
+        cand_sb = load_list(cand, "cand_sb")
+        gs_sb = keep.tile([P, PACK], F32, name="gs_sb")
+        nc.sync.dma_start(gs_sb[:], gs.rearrange("(p t) o -> p (t o)", t=PACK))
+        w_raw = keep.tile([P, PACK, H], F32, name="w_raw")
+        nc.sync.dma_start(w_raw[:], w1.rearrange("(p j) c -> p j c", j=PACK))
+        table_words = keep.tile([P, T], I32, name="table_words")
+        nc.sync.dma_start(table_words[:], x_words[0].rearrange("p n t -> p (n t)").bitcast(I32))
+        n2_sb = load_list(n2, "n2_sb")
+        n1_sb = load_list(n1, "n1_sb")
+        n3_sb = load_list(n3, "n3_sb")
+
+        x_planes = keep.tile([P, S + C], U8, name="x_planes", align_bytes=64)
+        nc.gpsimd.memset(x_planes[:], 0)
+        pages = []
+        for t in range(PACK):
+            page = keep.tile([P, U], F32, name=f"page{t}")
+            (nc.vector if t < 2 else nc.gpsimd).memset(page[:], 0.0)
+            pages.append(page)
+        scores = []
+        for c in range(C // P):
+            score = keep.tile([P, U + SPARE], F32, name=f"score{c}")
+            nc.gpsimd.memset(score[:, U:], 0.0)
+            scores.append(score)
+        neg_gs = keep.tile([P, PACK], F32, name="neg_gs")
+        nc.scalar.activation(neg_gs[:], gs_sb[:], ACT.Copy, scale=-1.0)
+
+        picked_scales = keep.tile([P, S + C], U8, name="picked_scales")
+        nc.vector.tensor_copy(picked_scales[:, :S], table_scales[:].indirect(offs_sb[:]))
+        nc.vector.tensor_copy(picked_scales[:, S:], table_scales[:].indirect(cand_sb[:]))
+        for j in range(4):
+            nc.scalar.dma_start(x_planes[:].bitcast(I32)[j:P:32, :], picked_scales[:].bitcast(I32)[8 * j : P : 32, :])
+
+        w_grouped = keep.tile([P, PACK * H], BF16, name="w_grouped", align_bytes=64)
+        nc.vector.tensor_copy(
+            w_grouped[:].rearrange("p (t m j) -> p m t j", t=PACK, j=PACK),
+            w_raw[:].rearrange("p j (m t) -> p m t j", t=PACK),
+        )
+        w_codes = keep.tile([P, H], U32, name="w_codes", align_bytes=64)
+        w_plane = keep.tile([P, H], U8, name="w_plane", align_bytes=64)
+        nc.vector.quantize_mx(out=w_codes[:].bitcast(FP8X4), scales=w_plane[:], in_=w_grouped[:])
+
+        place_words = keep.tile([P, S], U32, name="place_words", align_bytes=64)
+        nc.vector.tensor_copy(place_words[:], table_words[:].bitcast(U32).indirect(offs_sb[:]))
+        cand_words = keep.tile([P, C], U32, name="cand_words", align_bytes=64)
+        nc.vector.tensor_copy(cand_words[:], table_words[:].bitcast(U32).indirect(cand_sb[:]))
+
+        z_rows = keep.tile([P, PACK, U], BF16, name="z_rows")
+        half = S // 2
+        for t in range(PACK):
+            cols = slice(P * t, P * (t + 1))
+            y = psum.tile([P, BANK], F32, name="acc")
+            nc.tensor.matmul_mx(
+                out=y[:], lhsT=w_codes[:, cols].bitcast(FP8X4), lhsT_scale=w_plane[:, cols],
+                rhs=place_words[:].bitcast(FP8X4), rhs_scale=x_planes[:, :S], start=True, stop=True,
+            )
+            positive = keep.tile([P, S], F32, name=f"positive{t}")
+            nc.scalar.activation(positive[:], y[:], ACT.Relu)
+            negated = keep.tile([P, S], F32, name=f"negated{t}")
+            if t == 0:
+                nc.vector.tensor_scalar(negated[:], y[:], -1.0, None, ALU.mult)
+            else:
+                nc.scalar.activation(negated[:], y[:], ACT.Copy, scale=-1.0)
+            fetched = keep.tile([P, S], F32, name=f"fetched{t}")
+            for h in range(2):
+                entries = n2_sb[:, h * half // STRIPE : (h + 1) * half // STRIPE]
+                nc.scalar.activation(fetched[:, h * half : (h + 1) * half], positive[:].indirect(entries), ACT.Copy)
+            nc.vector.tensor_tensor(pages[t][:].indirect(n1_sb[:]), fetched[:], negated[:], ALU.add)
+        for t in range(PACK):
+            if t < PACK - 1:
+                nc.scalar.activation(z_rows[:, t, :], pages[t][:], ACT.Copy, scale=neg_gs[:, t : t + 1])
+            else:
+                nc.vector.tensor_scalar(z_rows[:, t, :], pages[t][:], neg_gs[:, t : t + 1], None, ALU.mult)
+
+        z_codes = keep.tile([P, U], U32, name="z_codes", align_bytes=64)
+        z_plane = keep.tile([P, U], U8, name="z_plane", align_bytes=64)
+
+        def weave(copy, grouped, first, lo, hi):
+            copy(
+                grouped[:, PACK * (lo - first) : PACK * (hi - first)].rearrange("p (c i t) -> p c t i", i=4, t=PACK),
+                z_rows[:, :, lo:hi].rearrange("p t (c i) -> p c t i", i=4),
+            )
+
+        z_low = keep.tile([P, PACK * BANK], BF16, name="z_low", align_bytes=64)
+        z_high = keep.tile([P, PACK * BANK], BF16, name="z_high", align_bytes=64)
+        weave(nc.vector.tensor_copy, z_low, 0, 0, BANK)
+        weave(nc.scalar.copy, z_high, BANK, U - Z_SCALAR_COLS, U)
+        weave(nc.vector.tensor_copy, z_high, BANK, BANK, U - Z_SCALAR_COLS)
+        for b, grouped in enumerate((z_low, z_high)):
+            cols = slice(BANK * b, BANK * (b + 1))
+            nc.vector.quantize_mx(out=z_codes[:, cols].bitcast(FP8X4), scales=z_plane[:, cols], in_=grouped[:])
+
+        for c in range(C // P):
+            rows_c = slice(P * c, P * (c + 1))
+            for b in range(U // BANK):
+                cols = slice(BANK * b, BANK * (b + 1))
+                acc = psum.tile([P, BANK], F32, name="acc")
+                nc.tensor.matmul_mx(
+                    out=acc[:], lhsT=cand_words[:, rows_c].bitcast(FP8X4), lhsT_scale=x_planes[:, S + P * c : S + P * (c + 1)],
+                    rhs=z_codes[:, cols].bitcast(FP8X4), rhs_scale=z_plane[:, cols], start=True, stop=True,
+                )
+                if c == 0 and b == 1:
+                    nc.vector.tensor_scalar(scores[c][:, cols], acc[:], 0.0625, None, ALU.mult)
+                else:
+                    nc.scalar.activation(scores[c][:, cols], acc[:], ACT.Copy, scale=0.0625)
+            members = keep.tile([P, W], F32, name=f"members{c}")
+            for q in range(W // PIECE):
+                looked_up = scores[c][:].indirect(n3_sb[:, q * PIECE // STRIPE : (q + 1) * PIECE // STRIPE])
+                if c == 0 and q < 2:
+                    nc.vector.tensor_copy(members[:, q * PIECE : (q + 1) * PIECE], looked_up)
+                else:
+                    nc.scalar.activation(members[:, q * PIECE : (q + 1) * PIECE], looked_up, ACT.Copy)
+            unit = PIECE if c == C // P - 1 else 2 * PIECE
+            for e0 in range(0, W, unit):
+                n = unit // MEMBERS
+                groups = members[:, e0 : e0 + unit].rearrange("p (w m) -> p w m", m=MEMBERS)
+                high = ring.tile([P, n, 2], F32, name="high")
+                low = ring.tile([P, n, 2], F32, name="low")
+                nc.vector.tensor_tensor(high[:], groups[:, :, 0:2], groups[:, :, 2:4], ALU.max)
+                nc.vector.tensor_tensor(low[:], groups[:, :, 0:2], groups[:, :, 2:4], ALU.min)
+                largest = ring.tile([P, n], F32, name="largest")
+                smallest = ring.tile([P, n], F32, name="smallest")
+                nc.vector.tensor_tensor(largest[:], high[:, :, 0], high[:, :, 1], ALU.max)
+                nc.vector.tensor_tensor(smallest[:], low[:, :, 0], low[:, :, 1], ALU.min)
+                result = ring.tile([P, n], F32, name="result", bufs=3)
+                nc.vector.scalar_tensor_tensor(result[:], smallest[:], -0.5, largest[:], ALU.mult, ALU.add)
+                w0 = e0 // MEMBERS
+                nc.sync.dma_start(out[rows_c, w0 : w0 + n], result[:])

@@ -20,7 +20,7 @@ STRIPE = 16
 BANK = 512
 SPARE = 32
 PIECE = 1024
-Z_SCALAR_COLS = 384
+Z_SCALAR_FROM = 576
 
 FLOPS = 2 * K * H * S + 2 * K * C * U
 
@@ -54,7 +54,7 @@ def tile_picked_hcandpagezgspan_none_p_kernel(tc, x_words, x_scales, w1, gs, off
         n3_sb = load_list(n3, "n3_sb")
 
         x_planes = keep.tile([P, S + C], U8, name="x_planes", align_bytes=64)
-        nc.gpsimd.memset(x_planes[:], 0)
+        nc.gpsimd.memset(x_planes[:].bitcast(I32), 0)
         pages = []
         for t in range(PACK):
             page = keep.tile([P, U], F32, name=f"page{t}")
@@ -72,7 +72,7 @@ def tile_picked_hcandpagezgspan_none_p_kernel(tc, x_words, x_scales, w1, gs, off
         nc.vector.tensor_copy(picked_scales[:, :S], table_scales[:].indirect(offs_sb[:]))
         nc.vector.tensor_copy(picked_scales[:, S:], table_scales[:].indirect(cand_sb[:]))
         for j in range(4):
-            nc.scalar.dma_start(x_planes[:].bitcast(I32)[j:P:32, :], picked_scales[:].bitcast(I32)[8 * j : P : 32, :])
+            nc.sync.dma_start(x_planes[:].bitcast(I32)[j:P:32, :], picked_scales[:].bitcast(I32)[8 * j : P : 32, :])
 
         w_grouped = keep.tile([P, PACK * H], BF16, name="w_grouped", align_bytes=64)
         nc.vector.tensor_copy(
@@ -84,36 +84,48 @@ def tile_picked_hcandpagezgspan_none_p_kernel(tc, x_words, x_scales, w1, gs, off
         nc.vector.quantize_mx(out=w_codes[:].bitcast(FP8X4), scales=w_plane[:], in_=w_grouped[:])
 
         place_words = keep.tile([P, S], U32, name="place_words", align_bytes=64)
-        nc.vector.tensor_copy(place_words[:], table_words[:].bitcast(U32).indirect(offs_sb[:]))
+        half = S // 2
+        for e0 in (0, half):
+            nc.vector.tensor_copy(
+                place_words[:, e0 : e0 + half], table_words[:].bitcast(U32).indirect(offs_sb[:, e0 // STRIPE : (e0 + half) // STRIPE])
+            )
         cand_words = keep.tile([P, C], U32, name="cand_words", align_bytes=64)
         nc.vector.tensor_copy(cand_words[:], table_words[:].bitcast(U32).indirect(cand_sb[:]))
 
         z_rows = keep.tile([P, PACK, U], BF16, name="z_rows")
-        half = S // 2
         for t in range(PACK):
             cols = slice(P * t, P * (t + 1))
-            y = psum.tile([P, BANK], F32, name="acc")
-            nc.tensor.matmul_mx(
-                out=y[:], lhsT=w_codes[:, cols].bitcast(FP8X4), lhsT_scale=w_plane[:, cols],
-                rhs=place_words[:].bitcast(FP8X4), rhs_scale=x_planes[:, :S], start=True, stop=True,
-            )
             positive = keep.tile([P, S], F32, name=f"positive{t}")
-            nc.scalar.activation(positive[:], y[:], ACT.Relu)
             negated = keep.tile([P, S], F32, name=f"negated{t}")
-            if t == 0:
-                nc.vector.tensor_scalar(negated[:], y[:], -1.0, None, ALU.mult)
-            else:
-                nc.scalar.activation(negated[:], y[:], ACT.Copy, scale=-1.0)
+            width = half if t == 0 else S
+            for e0 in range(0, S, width):
+                places = slice(e0, e0 + width)
+                y = psum.tile([P, width], F32, name="acc")
+                nc.tensor.matmul_mx(
+                    out=y[:], lhsT=w_codes[:, cols].bitcast(FP8X4), lhsT_scale=w_plane[:, cols],
+                    rhs=place_words[:, places].bitcast(FP8X4), rhs_scale=x_planes[:, places], start=True, stop=True,
+                )
+                nc.scalar.activation(positive[:, places], y[:], ACT.Relu)
+                if t == 0:
+                    nc.vector.tensor_scalar(negated[:, places], y[:], -1.0, None, ALU.mult)
+                else:
+                    nc.scalar.activation(negated[:, places], y[:], ACT.Copy, scale=-1.0)
             fetched = keep.tile([P, S], F32, name=f"fetched{t}")
             for h in range(2):
                 entries = n2_sb[:, h * half // STRIPE : (h + 1) * half // STRIPE]
                 nc.scalar.activation(fetched[:, h * half : (h + 1) * half], positive[:].indirect(entries), ACT.Copy)
-            nc.vector.tensor_tensor(pages[t][:].indirect(n1_sb[:]), fetched[:], negated[:], ALU.add)
-        for t in range(PACK):
-            if t < PACK - 1:
-                nc.scalar.activation(z_rows[:, t, :], pages[t][:], ACT.Copy, scale=neg_gs[:, t : t + 1])
-            else:
-                nc.vector.tensor_scalar(z_rows[:, t, :], pages[t][:], neg_gs[:, t : t + 1], None, ALU.mult)
+            for e0 in range(0, S, width):
+                entries = n1_sb[:, e0 // STRIPE : (e0 + width) // STRIPE]
+                nc.vector.tensor_tensor(pages[t][:].indirect(entries), fetched[:, e0 : e0 + width], negated[:, e0 : e0 + width], ALU.add)
+        for t in range(PACK - 1):
+            nc.scalar.activation(z_rows[:, t, :], pages[t][:], ACT.Copy, scale=neg_gs[:, t : t + 1])
+        last = PACK - 1
+        split = Z_SCALAR_FROM
+        quarter = U // 4
+        for lo, hi in ((0, quarter), (quarter, split)):
+            nc.vector.tensor_scalar(z_rows[:, last, lo:hi], pages[last][:, lo:hi], neg_gs[:, last:], None, ALU.mult)
+        for lo, hi in ((split, 3 * quarter), (3 * quarter, U)):
+            nc.scalar.activation(z_rows[:, last, lo:hi], pages[last][:, lo:hi], ACT.Copy, scale=neg_gs[:, last:])
 
         z_codes = keep.tile([P, U], U32, name="z_codes", align_bytes=64)
         z_plane = keep.tile([P, U], U8, name="z_plane", align_bytes=64)
@@ -126,46 +138,59 @@ def tile_picked_hcandpagezgspan_none_p_kernel(tc, x_words, x_scales, w1, gs, off
 
         z_low = keep.tile([P, PACK * BANK], BF16, name="z_low", align_bytes=64)
         z_high = keep.tile([P, PACK * BANK], BF16, name="z_high", align_bytes=64)
-        weave(nc.vector.tensor_copy, z_low, 0, 0, BANK)
-        weave(nc.scalar.copy, z_high, BANK, U - Z_SCALAR_COLS, U)
-        weave(nc.vector.tensor_copy, z_high, BANK, BANK, U - Z_SCALAR_COLS)
-        for b, grouped in enumerate((z_low, z_high)):
-            cols = slice(BANK * b, BANK * (b + 1))
-            nc.vector.quantize_mx(out=z_codes[:, cols].bitcast(FP8X4), scales=z_plane[:, cols], in_=grouped[:])
+
+        def quantise(grouped, first, lo, hi):
+            nc.vector.quantize_mx(
+                out=z_codes[:, lo:hi].bitcast(FP8X4), scales=z_plane[:, lo:hi], in_=grouped[:, PACK * (lo - first) : PACK * (hi - first)]
+            )
+
+        weave(nc.scalar.copy, z_high, BANK, split, 3 * quarter)
+        weave(nc.scalar.copy, z_high, BANK, 3 * quarter, U)
+        weave(nc.vector.tensor_copy, z_low, 0, 0, quarter)
+        weave(nc.vector.tensor_copy, z_low, 0, quarter, BANK)
+        weave(nc.vector.tensor_copy, z_high, BANK, BANK, split)
+        quantise(z_low, 0, 0, BANK)
+        quantise(z_high, BANK, BANK, 3 * quarter)
+        quantise(z_high, BANK, 3 * quarter, U)
 
         for c in range(C // P):
             rows_c = slice(P * c, P * (c + 1))
-            for b in range(U // BANK):
-                cols = slice(BANK * b, BANK * (b + 1))
-                acc = psum.tile([P, BANK], F32, name="acc")
+            edges = (0, BANK, 3 * quarter, U) if c == 0 else (0, BANK, U)
+            for lo, hi in zip(edges, edges[1:]):
+                cols = slice(lo, hi)
+                acc = psum.tile([P, hi - lo], F32, name="acc")
                 nc.tensor.matmul_mx(
                     out=acc[:], lhsT=cand_words[:, rows_c].bitcast(FP8X4), lhsT_scale=x_planes[:, S + P * c : S + P * (c + 1)],
                     rhs=z_codes[:, cols].bitcast(FP8X4), rhs_scale=z_plane[:, cols], start=True, stop=True,
                 )
-                if c == 0 and b == 1:
+                if c == 0 and lo > 0:
                     nc.vector.tensor_scalar(scores[c][:, cols], acc[:], 0.0625, None, ALU.mult)
                 else:
                     nc.scalar.activation(scores[c][:, cols], acc[:], ACT.Copy, scale=0.0625)
             members = keep.tile([P, W], F32, name=f"members{c}")
-            for q in range(W // PIECE):
-                looked_up = scores[c][:].indirect(n3_sb[:, q * PIECE // STRIPE : (q + 1) * PIECE // STRIPE])
-                if c == 0 and q < 2:
-                    nc.vector.tensor_copy(members[:, q * PIECE : (q + 1) * PIECE], looked_up)
+            for p0 in range(0, W, PIECE):
+                looked_up = scores[c][:].indirect(n3_sb[:, p0 // STRIPE : (p0 + PIECE) // STRIPE])
+                if c == 0 and p0 < W // 2:
+                    nc.vector.tensor_copy(members[:, p0 : p0 + PIECE], looked_up)
                 else:
-                    nc.scalar.activation(members[:, q * PIECE : (q + 1) * PIECE], looked_up, ACT.Copy)
-            unit = PIECE if c == C // P - 1 else 2 * PIECE
-            for e0 in range(0, W, unit):
-                n = unit // MEMBERS
-                groups = members[:, e0 : e0 + unit].rearrange("p (w m) -> p w m", m=MEMBERS)
-                high = ring.tile([P, n, 2], F32, name="high")
-                low = ring.tile([P, n, 2], F32, name="low")
-                nc.vector.tensor_tensor(high[:], groups[:, :, 0:2], groups[:, :, 2:4], ALU.max)
-                nc.vector.tensor_tensor(low[:], groups[:, :, 0:2], groups[:, :, 2:4], ALU.min)
-                largest = ring.tile([P, n], F32, name="largest")
-                smallest = ring.tile([P, n], F32, name="smallest")
-                nc.vector.tensor_tensor(largest[:], high[:, :, 0], high[:, :, 1], ALU.max)
-                nc.vector.tensor_tensor(smallest[:], low[:, :, 0], low[:, :, 1], ALU.min)
-                result = ring.tile([P, n], F32, name="result", bufs=3)
+                    nc.scalar.activation(members[:, p0 : p0 + PIECE], looked_up, ACT.Copy)
+            groups = members[:].rearrange("p (w m) -> p w m", m=MEMBERS)
+            high = ring.tile([P, 2 * U], F32, name="high")
+            low = ring.tile([P, 2 * U], F32, name="low")
+            high_pairs = high[:].rearrange("p (w m) -> p w m", m=2)
+            low_pairs = low[:].rearrange("p (w m) -> p w m", m=2)
+            paired, finished = (quarter, quarter) if c == C // P - 1 else (BANK, U if c == 0 else BANK)
+            for w0 in range(0, U, paired):
+                cols = slice(w0, w0 + paired)
+                nc.vector.tensor_tensor(high_pairs[:, cols, :], groups[:, cols, 0:2], groups[:, cols, 2:4], ALU.max)
+                nc.vector.tensor_tensor(low_pairs[:, cols, :], groups[:, cols, 0:2], groups[:, cols, 2:4], ALU.min)
+                if (w0 + paired) % finished:
+                    continue
+                cols = slice(w0 + paired - finished, w0 + paired)
+                largest = ring.tile([P, finished], F32, name="largest")
+                smallest = ring.tile([P, finished], F32, name="smallest")
+                nc.vector.tensor_tensor(largest[:], high_pairs[:, cols, 0], high_pairs[:, cols, 1], ALU.max)
+                nc.vector.tensor_tensor(smallest[:], low_pairs[:, cols, 0], low_pairs[:, cols, 1], ALU.min)
+                result = ring.tile([P, finished], F32, name="result", bufs=3)
                 nc.vector.scalar_tensor_tensor(result[:], smallest[:], -0.5, largest[:], ALU.mult, ALU.add)
-                w0 = e0 // MEMBERS
-                nc.sync.dma_start(out[rows_c, w0 : w0 + n], result[:])
+                nc.sync.dma_start(out[rows_c, cols], result[:])

@@ -31,7 +31,7 @@ def tile_picked_hcandpagezgspan_none_p_kernel(tc, x_words, x_scales, w1, gs, off
         lists = ctx.enter_context(tc.tile_pool(name="lists", bufs=1))
         keep = ctx.enter_context(tc.tile_pool(name="keep", bufs=1))
         ring = ctx.enter_context(tc.tile_pool(name="ring", bufs=2))
-        psum = ctx.enter_context(tc.psum_pool(name="psum", bufs=8))
+        psum = ctx.enter_context(tc.psum_pool(name="psum", bufs=1))
 
         def load_list(src, name):
             tile = lists.tile(list(src.shape), U16, name=name)
@@ -100,7 +100,7 @@ def tile_picked_hcandpagezgspan_none_p_kernel(tc, x_words, x_scales, w1, gs, off
             width = half if t == 0 else S
             for e0 in range(0, S, width):
                 places = slice(e0, e0 + width)
-                y = psum.tile([P, width], F32, name="acc")
+                y = psum.tile([P, width], F32, name="y", bufs=2)
                 nc.tensor.matmul_mx(
                     out=y[:], lhsT=w_codes[:, cols].bitcast(FP8X4), lhsT_scale=w_plane[:, cols],
                     rhs=place_words[:, places].bitcast(FP8X4), rhs_scale=x_planes[:, places], start=True, stop=True,
@@ -158,7 +158,7 @@ def tile_picked_hcandpagezgspan_none_p_kernel(tc, x_words, x_scales, w1, gs, off
             edges = (0, BANK, 3 * quarter, U) if c == 0 else (0, BANK, U)
             for lo, hi in zip(edges, edges[1:]):
                 cols = slice(lo, hi)
-                acc = psum.tile([P, hi - lo], F32, name="acc")
+                acc = psum.tile([P, hi - lo], F32, name="acc", bufs=6)
                 nc.tensor.matmul_mx(
                     out=acc[:], lhsT=cand_words[:, rows_c].bitcast(FP8X4), lhsT_scale=x_planes[:, S + P * c : S + P * (c + 1)],
                     rhs=z_codes[:, cols].bitcast(FP8X4), rhs_scale=z_plane[:, cols], start=True, stop=True,
@@ -179,14 +179,18 @@ def tile_picked_hcandpagezgspan_none_p_kernel(tc, x_words, x_scales, w1, gs, off
             low = ring.tile([P, 2 * U], F32, name="low")
             high_pairs = high[:].rearrange("p (w m) -> p w m", m=2)
             low_pairs = low[:].rearrange("p (w m) -> p w m", m=2)
-            paired, finished = (quarter, quarter) if c == C // P - 1 else (BANK, U if c == 0 else BANK)
+            paired = quarter if c == C // P - 1 else BANK
+            ends = ((U,), (U,), (BANK, U), (BANK, 3 * quarter, U))[c]
+            done = 0
             for w0 in range(0, U, paired):
                 cols = slice(w0, w0 + paired)
                 nc.vector.tensor_tensor(high_pairs[:, cols, :], groups[:, cols, 0:2], groups[:, cols, 2:4], ALU.max)
                 nc.vector.tensor_tensor(low_pairs[:, cols, :], groups[:, cols, 0:2], groups[:, cols, 2:4], ALU.min)
-                if (w0 + paired) % finished:
+                if w0 + paired not in ends:
                     continue
-                cols = slice(w0 + paired - finished, w0 + paired)
+                cols = slice(done, w0 + paired)
+                finished = w0 + paired - done
+                done = w0 + paired
                 largest = ring.tile([P, finished], F32, name="largest")
                 smallest = ring.tile([P, finished], F32, name="smallest")
                 nc.vector.tensor_tensor(largest[:], high_pairs[:, cols, 0], high_pairs[:, cols, 1], ALU.max)

@@ -12,35 +12,49 @@ FP8X4 = mybir.dt.float8_e4m3fn_x4
 ALU = mybir.AluOpType
 ACT = mybir.ActivationFunctionType
 
+K, T, S, H, U, C, W = 512, 2048, 512, 512, 1024, 512, 4096
 P = 128
 PACK = 4
-K, T, S, H, U, C, W = 512, 2048, 512, 512, 1024, 512, 4096
+BLOCKS = K // 32
+QUADRANT = 32
+PLANE_ROWS = 4
+BLOCK_PARTITIONS = P // BLOCKS
+SCORE_SCALE = 0.0625
 MEMBERS = 4
 STRIPE = 16
 BANK = 512
-SPARE = 32
 PIECE = 1024
+SPARE = 32
+WALK = 4
 Z_SCALAR_FROM = 576
+VECTOR_ENTRIES = 2688
 
 FLOPS = 2 * K * H * S + 2 * K * C * U
 
 
 def tile_picked_hcandpagezgspan_none_p_kernel(tc, x_words, x_scales, w1, gs, offs, n1, n2, cand, n3, out):
     nc = tc.nc
+    half_places = S // 2
+    quarter = U // 4
+    cand_tiles = C // P
+
+    def entries(list_tile, first, end):
+        return list_tile[:, first // STRIPE : end // STRIPE]
+
     with ExitStack() as ctx:
         lists = ctx.enter_context(tc.tile_pool(name="lists", bufs=1))
         keep = ctx.enter_context(tc.tile_pool(name="keep", bufs=1))
         ring = ctx.enter_context(tc.tile_pool(name="ring", bufs=2))
         psum = ctx.enter_context(tc.psum_pool(name="psum", bufs=1))
 
-        def load_list(src, name):
-            tile = lists.tile(list(src.shape), U16, name=name)
-            nc.sync.dma_start(tile[:], src)
+        def load_list(source, name):
+            tile = lists.tile(list(source.shape), U16, name=name)
+            nc.sync.dma_start(tile[:], source)
             return tile
 
         table_scales = keep.tile([P, T], U8, name="table_scales")
-        rows = x_scales[0].bitcast(I32)
-        nc.sync.dma_start(table_scales[:].bitcast(I32), rows.unsqueeze(1).to_broadcast([16, 8, T // 4]))
+        scale_rows = x_scales[0].bitcast(I32)
+        nc.sync.dma_start(table_scales[:].bitcast(I32), scale_rows.unsqueeze(1).to_broadcast([BLOCKS, BLOCK_PARTITIONS, scale_rows.shape[1]]))
         offs_sb = load_list(offs, "offs_sb")
         cand_sb = load_list(cand, "cand_sb")
         gs_sb = keep.tile([P, PACK], F32, name="gs_sb")
@@ -58,10 +72,10 @@ def tile_picked_hcandpagezgspan_none_p_kernel(tc, x_words, x_scales, w1, gs, off
         pages = []
         for t in range(PACK):
             page = keep.tile([P, U], F32, name=f"page{t}")
-            (nc.vector if t < 2 else nc.gpsimd).memset(page[:], 0.0)
+            (nc.vector if t < PACK // 2 else nc.gpsimd).memset(page[:], 0.0)
             pages.append(page)
         scores = []
-        for c in range(C // P):
+        for c in range(cand_tiles):
             score = keep.tile([P, U + SPARE], F32, name=f"score{c}")
             nc.gpsimd.memset(score[:, U:], 0.0)
             scores.append(score)
@@ -71,8 +85,11 @@ def tile_picked_hcandpagezgspan_none_p_kernel(tc, x_words, x_scales, w1, gs, off
         picked_scales = keep.tile([P, S + C], U8, name="picked_scales")
         nc.vector.tensor_copy(picked_scales[:, :S], table_scales[:].indirect(offs_sb[:]))
         nc.vector.tensor_copy(picked_scales[:, S:], table_scales[:].indirect(cand_sb[:]))
-        for j in range(4):
-            nc.sync.dma_start(x_planes[:].bitcast(I32)[j:P:32, :], picked_scales[:].bitcast(I32)[8 * j : P : 32, :])
+        for j in range(PLANE_ROWS):
+            nc.sync.dma_start(
+                x_planes[:].bitcast(I32)[j:P:QUADRANT, :],
+                picked_scales[:].bitcast(I32)[BLOCK_PARTITIONS * j : P : QUADRANT, :],
+            )
 
         w_grouped = keep.tile([P, PACK * H], BF16, name="w_grouped", align_bytes=64)
         nc.vector.tensor_copy(
@@ -84,26 +101,29 @@ def tile_picked_hcandpagezgspan_none_p_kernel(tc, x_words, x_scales, w1, gs, off
         nc.vector.quantize_mx(out=w_codes[:].bitcast(FP8X4), scales=w_plane[:], in_=w_grouped[:])
 
         place_words = keep.tile([P, S], U32, name="place_words", align_bytes=64)
-        half = S // 2
-        for e0 in (0, half):
-            nc.vector.tensor_copy(
-                place_words[:, e0 : e0 + half], table_words[:].bitcast(U32).indirect(offs_sb[:, e0 // STRIPE : (e0 + half) // STRIPE])
-            )
+        for first in (0, half_places):
+            end = first + half_places
+            nc.vector.tensor_copy(place_words[:, first:end], table_words[:].bitcast(U32).indirect(entries(offs_sb, first, end)))
         cand_words = keep.tile([P, C], U32, name="cand_words", align_bytes=64)
         nc.vector.tensor_copy(cand_words[:], table_words[:].bitcast(U32).indirect(cand_sb[:]))
 
         z_rows = keep.tile([P, PACK, U], BF16, name="z_rows")
         for t in range(PACK):
-            cols = slice(P * t, P * (t + 1))
+            w_cols = slice(P * t, P * (t + 1))
             positive = keep.tile([P, S], F32, name=f"positive{t}")
             negated = keep.tile([P, S], F32, name=f"negated{t}")
-            width = half if t == 0 else S
-            for e0 in range(0, S, width):
-                places = slice(e0, e0 + width)
-                y = psum.tile([P, width], F32, name="y", bufs=2)
+            step = half_places if t == 0 else S
+            for first in range(0, S, step):
+                places = slice(first, first + step)
+                y = psum.tile([P, step], F32, name="y", bufs=2)
                 nc.tensor.matmul_mx(
-                    out=y[:], lhsT=w_codes[:, cols].bitcast(FP8X4), lhsT_scale=w_plane[:, cols],
-                    rhs=place_words[:, places].bitcast(FP8X4), rhs_scale=x_planes[:, places], start=True, stop=True,
+                    out=y[:],
+                    lhsT=w_codes[:, w_cols].bitcast(FP8X4),
+                    lhsT_scale=w_plane[:, w_cols],
+                    rhs=place_words[:, places].bitcast(FP8X4),
+                    rhs_scale=x_planes[:, places],
+                    start=True,
+                    stop=True,
                 )
                 nc.scalar.activation(positive[:, places], y[:], ACT.Relu)
                 if t == 0:
@@ -111,90 +131,96 @@ def tile_picked_hcandpagezgspan_none_p_kernel(tc, x_words, x_scales, w1, gs, off
                 else:
                     nc.scalar.activation(negated[:, places], y[:], ACT.Copy, scale=-1.0)
             fetched = keep.tile([P, S], F32, name=f"fetched{t}")
-            for h in range(2):
-                entries = n2_sb[:, h * half // STRIPE : (h + 1) * half // STRIPE]
-                nc.scalar.activation(fetched[:, h * half : (h + 1) * half], positive[:].indirect(entries), ACT.Copy)
-            for e0 in range(0, S, width):
-                entries = n1_sb[:, e0 // STRIPE : (e0 + width) // STRIPE]
-                nc.vector.tensor_tensor(pages[t][:].indirect(entries), fetched[:, e0 : e0 + width], negated[:, e0 : e0 + width], ALU.add)
+            for first in (0, half_places):
+                end = first + half_places
+                nc.scalar.activation(fetched[:, first:end], positive[:].indirect(entries(n2_sb, first, end)), ACT.Copy)
+            for first in range(0, S, step):
+                end = first + step
+                nc.vector.tensor_tensor(
+                    pages[t][:].indirect(entries(n1_sb, first, end)), fetched[:, first:end], negated[:, first:end], ALU.add
+                )
+
         for t in range(PACK - 1):
             nc.scalar.activation(z_rows[:, t, :], pages[t][:], ACT.Copy, scale=neg_gs[:, t : t + 1])
         last = PACK - 1
-        split = Z_SCALAR_FROM
-        quarter = U // 4
-        for lo, hi in ((0, quarter), (quarter, split)):
+        for lo, hi in ((0, quarter), (quarter, Z_SCALAR_FROM)):
             nc.vector.tensor_scalar(z_rows[:, last, lo:hi], pages[last][:, lo:hi], neg_gs[:, last:], None, ALU.mult)
-        for lo, hi in ((split, 3 * quarter), (3 * quarter, U)):
+        for lo, hi in ((Z_SCALAR_FROM, 3 * quarter), (3 * quarter, U)):
             nc.scalar.activation(z_rows[:, last, lo:hi], pages[last][:, lo:hi], ACT.Copy, scale=neg_gs[:, last:])
 
         z_codes = keep.tile([P, U], U32, name="z_codes", align_bytes=64)
         z_plane = keep.tile([P, U], U8, name="z_plane", align_bytes=64)
-
-        def weave(copy, grouped, first, lo, hi):
-            copy(
-                grouped[:, PACK * (lo - first) : PACK * (hi - first)].rearrange("p (c i t) -> p c t i", i=4, t=PACK),
-                z_rows[:, :, lo:hi].rearrange("p t (c i) -> p c t i", i=4),
-            )
-
         z_low = keep.tile([P, PACK * BANK], BF16, name="z_low", align_bytes=64)
         z_high = keep.tile([P, PACK * BANK], BF16, name="z_high", align_bytes=64)
 
-        def quantise(grouped, first, lo, hi):
-            nc.vector.quantize_mx(
-                out=z_codes[:, lo:hi].bitcast(FP8X4), scales=z_plane[:, lo:hi], in_=grouped[:, PACK * (lo - first) : PACK * (hi - first)]
+        def grouped(lo, hi):
+            tile, base = (z_low, 0) if lo < BANK else (z_high, BANK)
+            return tile[:, PACK * (lo - base) : PACK * (hi - base)]
+
+        def interleave(copy, lo, hi):
+            copy(
+                grouped(lo, hi).rearrange("p (c i t) -> p c t i", i=WALK, t=PACK),
+                z_rows[:, :, lo:hi].rearrange("p t (c i) -> p c t i", i=WALK),
             )
 
-        weave(nc.scalar.copy, z_high, BANK, split, 3 * quarter)
-        weave(nc.scalar.copy, z_high, BANK, 3 * quarter, U)
-        weave(nc.vector.tensor_copy, z_low, 0, 0, quarter)
-        weave(nc.vector.tensor_copy, z_low, 0, quarter, BANK)
-        weave(nc.vector.tensor_copy, z_high, BANK, BANK, split)
-        quantise(z_low, 0, 0, BANK)
-        quantise(z_high, BANK, BANK, 3 * quarter)
-        quantise(z_high, BANK, 3 * quarter, U)
+        interleave(nc.scalar.copy, Z_SCALAR_FROM, 3 * quarter)
+        interleave(nc.scalar.copy, 3 * quarter, U)
+        interleave(nc.vector.tensor_copy, 0, quarter)
+        interleave(nc.vector.tensor_copy, quarter, BANK)
+        interleave(nc.vector.tensor_copy, BANK, Z_SCALAR_FROM)
+        z_edges = (0, BANK, 3 * quarter, U)
+        for lo, hi in zip(z_edges, z_edges[1:]):
+            nc.vector.quantize_mx(out=z_codes[:, lo:hi].bitcast(FP8X4), scales=z_plane[:, lo:hi], in_=grouped(lo, hi))
 
-        for c in range(C // P):
-            rows_c = slice(P * c, P * (c + 1))
-            edges = (0, BANK, 3 * quarter, U) if c == 0 else (0, BANK, U)
-            for lo, hi in zip(edges, edges[1:]):
-                cols = slice(lo, hi)
+        for c in range(cand_tiles):
+            first_tile, last_tile = c == 0, c == cand_tiles - 1
+            cands = slice(P * c, P * (c + 1))
+            s_edges = z_edges if first_tile else (0, BANK, U)
+            for lo, hi in zip(s_edges, s_edges[1:]):
                 acc = psum.tile([P, hi - lo], F32, name="acc", bufs=6)
                 nc.tensor.matmul_mx(
-                    out=acc[:], lhsT=cand_words[:, rows_c].bitcast(FP8X4), lhsT_scale=x_planes[:, S + P * c : S + P * (c + 1)],
-                    rhs=z_codes[:, cols].bitcast(FP8X4), rhs_scale=z_plane[:, cols], start=True, stop=True,
+                    out=acc[:],
+                    lhsT=cand_words[:, cands].bitcast(FP8X4),
+                    lhsT_scale=x_planes[:, S + P * c : S + P * (c + 1)],
+                    rhs=z_codes[:, lo:hi].bitcast(FP8X4),
+                    rhs_scale=z_plane[:, lo:hi],
+                    start=True,
+                    stop=True,
                 )
-                if c == 0 and lo > 0:
-                    nc.vector.tensor_scalar(scores[c][:, cols], acc[:], 0.0625, None, ALU.mult)
+                if first_tile and lo > 0:
+                    nc.vector.tensor_scalar(scores[c][:, lo:hi], acc[:], SCORE_SCALE, None, ALU.mult)
                 else:
-                    nc.scalar.activation(scores[c][:, cols], acc[:], ACT.Copy, scale=0.0625)
+                    nc.scalar.activation(scores[c][:, lo:hi], acc[:], ACT.Copy, scale=SCORE_SCALE)
+
             members = keep.tile([P, W], F32, name=f"members{c}")
-            for p0 in range(0, W, PIECE):
-                looked_up = scores[c][:].indirect(n3_sb[:, p0 // STRIPE : (p0 + PIECE) // STRIPE])
-                if c == 0 and p0 < W // 2:
-                    nc.vector.tensor_copy(members[:, p0 : p0 + PIECE], looked_up)
-                else:
-                    nc.scalar.activation(members[:, p0 : p0 + PIECE], looked_up, ACT.Copy)
+            border = VECTOR_ENTRIES if first_tile else 0
+            for first in range(0, border, PIECE):
+                end = min(first + PIECE, border)
+                nc.vector.tensor_copy(members[:, first:end], scores[c][:].indirect(entries(n3_sb, first, end)))
+            cuts = list(range(border, W, PIECE)) + ([W - PIECE // 4] if last_tile else []) + [W]
+            for first, end in zip(cuts, cuts[1:]):
+                nc.scalar.activation(members[:, first:end], scores[c][:].indirect(entries(n3_sb, first, end)), ACT.Copy)
+
+            if first_tile:
+                stretch_ends = [U]
+            elif last_tile:
+                stretch_ends = [end // MEMBERS for end in cuts[1:]]
+            else:
+                stretch_ends = [BANK, U]
             groups = members[:].rearrange("p (w m) -> p w m", m=MEMBERS)
             high = ring.tile([P, 2 * U], F32, name="high")
             low = ring.tile([P, 2 * U], F32, name="low")
             high_pairs = high[:].rearrange("p (w m) -> p w m", m=2)
             low_pairs = low[:].rearrange("p (w m) -> p w m", m=2)
-            paired = quarter if c == C // P - 1 else BANK
-            ends = ((U,), (U,), (BANK, U), (BANK, 3 * quarter, U))[c]
-            done = 0
-            for w0 in range(0, U, paired):
-                cols = slice(w0, w0 + paired)
-                nc.vector.tensor_tensor(high_pairs[:, cols, :], groups[:, cols, 0:2], groups[:, cols, 2:4], ALU.max)
-                nc.vector.tensor_tensor(low_pairs[:, cols, :], groups[:, cols, 0:2], groups[:, cols, 2:4], ALU.min)
-                if w0 + paired not in ends:
-                    continue
-                cols = slice(done, w0 + paired)
-                finished = w0 + paired - done
-                done = w0 + paired
-                largest = ring.tile([P, finished], F32, name="largest")
-                smallest = ring.tile([P, finished], F32, name="smallest")
-                nc.vector.tensor_tensor(largest[:], high_pairs[:, cols, 0], high_pairs[:, cols, 1], ALU.max)
-                nc.vector.tensor_tensor(smallest[:], low_pairs[:, cols, 0], low_pairs[:, cols, 1], ALU.min)
-                result = ring.tile([P, finished], F32, name="result", bufs=3)
+            for lo, hi in zip([0] + stretch_ends, stretch_ends):
+                nc.vector.tensor_tensor(high_pairs[:, lo:hi, :], groups[:, lo:hi, 0:2], groups[:, lo:hi, 2:4], ALU.max)
+                nc.vector.tensor_tensor(low_pairs[:, lo:hi, :], groups[:, lo:hi, 0:2], groups[:, lo:hi, 2:4], ALU.min)
+                slots = slice(lo, hi)
+                width = hi - lo
+                largest = ring.tile([P, width], F32, name="largest")
+                smallest = ring.tile([P, width], F32, name="smallest")
+                nc.vector.tensor_tensor(largest[:], high_pairs[:, slots, 0], high_pairs[:, slots, 1], ALU.max)
+                nc.vector.tensor_tensor(smallest[:], low_pairs[:, slots, 0], low_pairs[:, slots, 1], ALU.min)
+                result = ring.tile([P, width], F32, name="result", bufs=3)
                 nc.vector.scalar_tensor_tensor(result[:], smallest[:], -0.5, largest[:], ALU.mult, ALU.add)
-                nc.sync.dma_start(out[rows_c, cols], result[:])
+                nc.sync.dma_start(out[cands, slots], result[:])

from contextlib import ExitStack

import concourse.mybir as mybir

F32 = mybir.dt.float32
BF16 = mybir.dt.bfloat16
I32 = mybir.dt.int32
U32 = mybir.dt.uint32
U16 = mybir.dt.uint16
U8 = mybir.dt.uint8
FP8X4 = mybir.dt.float8_e4m3fn_x4
ALU = mybir.AluOpType
ACT = mybir.ActivationFunctionType

K, T, S, H, U, C, W = 512, 2048, 512, 512, 1024, 512, 4096
P = 128
PACK = 4
BLOCKS = K // 32
QUADRANT = 32
PLANE_ROWS = 4
BLOCK_PARTITIONS = P // BLOCKS
SCORE_SCALE = 0.0625
MEMBERS = 4
STRIPE = 16
BANK = 512
PIECE = 1024
SPARE = 32
WALK = 4
Z_SCALAR_FROM = 576
VECTOR_ENTRIES = 2688

FLOPS = 2 * K * H * S + 2 * K * C * U


def tile_picked_hcandpagezgspan_none_p_kernel(tc, x_words, x_scales, w1, gs, offs, n1, n2, cand, n3, out):
    nc = tc.nc
    half_places = S // 2
    quarter = U // 4
    cand_tiles = C // P

    def entries(list_tile, first, end):
        return list_tile[:, first // STRIPE : end // STRIPE]

    with ExitStack() as ctx:
        lists = ctx.enter_context(tc.tile_pool(name="lists", bufs=1))
        keep = ctx.enter_context(tc.tile_pool(name="keep", bufs=1))
        ring = ctx.enter_context(tc.tile_pool(name="ring", bufs=2))
        psum = ctx.enter_context(tc.psum_pool(name="psum", bufs=1))

        def load_list(source, name):
            tile = lists.tile(list(source.shape), U16, name=name)
            nc.sync.dma_start(tile[:], source)
            return tile

        table_scales = keep.tile([P, T], U8, name="table_scales")
        scale_rows = x_scales[0].bitcast(I32)
        nc.sync.dma_start(table_scales[:].bitcast(I32), scale_rows.unsqueeze(1).to_broadcast([BLOCKS, BLOCK_PARTITIONS, scale_rows.shape[1]]))
        offs_sb = load_list(offs, "offs_sb")
        cand_sb = load_list(cand, "cand_sb")
        gs_sb = keep.tile([P, PACK], F32, name="gs_sb")
        nc.sync.dma_start(gs_sb[:], gs.rearrange("(p t) o -> p (t o)", t=PACK))
        w_raw = keep.tile([P, PACK, H], F32, name="w_raw")
        nc.sync.dma_start(w_raw[:], w1.rearrange("(p j) c -> p j c", j=PACK))
        table_words = keep.tile([P, T], I32, name="table_words")
        nc.sync.dma_start(table_words[:], x_words[0].rearrange("p n t -> p (n t)").bitcast(I32))
        n2_sb = load_list(n2, "n2_sb")
        n1_sb = load_list(n1, "n1_sb")
        n3_sb = load_list(n3, "n3_sb")

        x_planes = keep.tile([P, S + C], U8, name="x_planes", align_bytes=64)
        nc.gpsimd.memset(x_planes[:].bitcast(I32), 0)
        pages = []
        for t in range(PACK):
            page = keep.tile([P, U], F32, name=f"page{t}")
            (nc.vector if t < PACK // 2 else nc.gpsimd).memset(page[:], 0.0)
            pages.append(page)
        scores = []
        for c in range(cand_tiles):
            score = keep.tile([P, U + SPARE], F32, name=f"score{c}")
            nc.gpsimd.memset(score[:, U:], 0.0)
            scores.append(score)
        neg_gs = keep.tile([P, PACK], F32, name="neg_gs")
        nc.scalar.activation(neg_gs[:], gs_sb[:], ACT.Copy, scale=-1.0)

        picked_scales = keep.tile([P, S + C], U8, name="picked_scales")
        nc.vector.tensor_copy(picked_scales[:, :S], table_scales[:].indirect(offs_sb[:]))
        nc.vector.tensor_copy(picked_scales[:, S:], table_scales[:].indirect(cand_sb[:]))
        for j in range(PLANE_ROWS):
            nc.sync.dma_start(
                x_planes[:].bitcast(I32)[j:P:QUADRANT, :],
                picked_scales[:].bitcast(I32)[BLOCK_PARTITIONS * j : P : QUADRANT, :],
            )

        w_grouped = keep.tile([P, PACK * H], BF16, name="w_grouped", align_bytes=64)
        nc.vector.tensor_copy(
            w_grouped[:].rearrange("p (t m j) -> p m t j", t=PACK, j=PACK),
            w_raw[:].rearrange("p j (m t) -> p m t j", t=PACK),
        )
        w_codes = keep.tile([P, H], U32, name="w_codes", align_bytes=64)
        w_plane = keep.tile([P, H], U8, name="w_plane", align_bytes=64)
        nc.vector.quantize_mx(out=w_codes[:].bitcast(FP8X4), scales=w_plane[:], in_=w_grouped[:])

        place_words = keep.tile([P, S], U32, name="place_words", align_bytes=64)
        for first in (0, half_places):
            end = first + half_places
            nc.vector.tensor_copy(place_words[:, first:end], table_words[:].bitcast(U32).indirect(entries(offs_sb, first, end)))
        cand_words = keep.tile([P, C], U32, name="cand_words", align_bytes=64)
        nc.vector.tensor_copy(cand_words[:], table_words[:].bitcast(U32).indirect(cand_sb[:]))

        z_rows = keep.tile([P, PACK, U], BF16, name="z_rows")
        for t in range(PACK):
            w_cols = slice(P * t, P * (t + 1))
            positive = keep.tile([P, S], F32, name=f"positive{t}")
            negated = keep.tile([P, S], F32, name=f"negated{t}")
            step = half_places if t == 0 else S
            for first in range(0, S, step):
                places = slice(first, first + step)
                y = psum.tile([P, step], F32, name="y", bufs=2)
                nc.tensor.matmul_mx(
                    out=y[:],
                    lhsT=w_codes[:, w_cols].bitcast(FP8X4),
                    lhsT_scale=w_plane[:, w_cols],
                    rhs=place_words[:, places].bitcast(FP8X4),
                    rhs_scale=x_planes[:, places],
                    start=True,
                    stop=True,
                )
                nc.scalar.activation(positive[:, places], y[:], ACT.Relu)
                if t == 0:
                    nc.vector.tensor_scalar(negated[:, places], y[:], -1.0, None, ALU.mult)
                else:
                    nc.scalar.activation(negated[:, places], y[:], ACT.Copy, scale=-1.0)
            fetched = keep.tile([P, S], F32, name=f"fetched{t}")
            for first in (0, half_places):
                end = first + half_places
                nc.scalar.activation(fetched[:, first:end], positive[:].indirect(entries(n2_sb, first, end)), ACT.Copy)
            for first in range(0, S, step):
                end = first + step
                nc.vector.tensor_tensor(
                    pages[t][:].indirect(entries(n1_sb, first, end)), fetched[:, first:end], negated[:, first:end], ALU.add
                )

        for t in range(PACK - 1):
            nc.scalar.activation(z_rows[:, t, :], pages[t][:], ACT.Copy, scale=neg_gs[:, t : t + 1])
        last = PACK - 1
        for lo, hi in ((0, quarter), (quarter, Z_SCALAR_FROM)):
            nc.vector.tensor_scalar(z_rows[:, last, lo:hi], pages[last][:, lo:hi], neg_gs[:, last:], None, ALU.mult)
        for lo, hi in ((Z_SCALAR_FROM, 3 * quarter), (3 * quarter, U)):
            nc.scalar.activation(z_rows[:, last, lo:hi], pages[last][:, lo:hi], ACT.Copy, scale=neg_gs[:, last:])

        z_codes = keep.tile([P, U], U32, name="z_codes", align_bytes=64)
        z_plane = keep.tile([P, U], U8, name="z_plane", align_bytes=64)
        z_low = keep.tile([P, PACK * BANK], BF16, name="z_low", align_bytes=64)
        z_high = keep.tile([P, PACK * BANK], BF16, name="z_high", align_bytes=64)

        def grouped(lo, hi):
            tile, base = (z_low, 0) if lo < BANK else (z_high, BANK)
            return tile[:, PACK * (lo - base) : PACK * (hi - base)]

        def interleave(copy, lo, hi):
            copy(
                grouped(lo, hi).rearrange("p (c i t) -> p c t i", i=WALK, t=PACK),
                z_rows[:, :, lo:hi].rearrange("p t (c i) -> p c t i", i=WALK),
            )

        interleave(nc.scalar.copy, Z_SCALAR_FROM, 3 * quarter)
        interleave(nc.scalar.copy, 3 * quarter, U)
        interleave(nc.vector.tensor_copy, 0, quarter)
        interleave(nc.vector.tensor_copy, quarter, BANK)
        interleave(nc.vector.tensor_copy, BANK, Z_SCALAR_FROM)
        z_edges = (0, BANK, 3 * quarter, U)
        for lo, hi in zip(z_edges, z_edges[1:]):
            nc.vector.quantize_mx(out=z_codes[:, lo:hi].bitcast(FP8X4), scales=z_plane[:, lo:hi], in_=grouped(lo, hi))

        for c in range(cand_tiles):
            first_tile, last_tile = c == 0, c == cand_tiles - 1
            cands = slice(P * c, P * (c + 1))
            s_edges = z_edges if first_tile else (0, BANK, U)
            for lo, hi in zip(s_edges, s_edges[1:]):
                acc = psum.tile([P, hi - lo], F32, name="acc", bufs=6)
                nc.tensor.matmul_mx(
                    out=acc[:],
                    lhsT=cand_words[:, cands].bitcast(FP8X4),
                    lhsT_scale=x_planes[:, S + P * c : S + P * (c + 1)],
                    rhs=z_codes[:, lo:hi].bitcast(FP8X4),
                    rhs_scale=z_plane[:, lo:hi],
                    start=True,
                    stop=True,
                )
                if first_tile and lo > 0:
                    nc.vector.tensor_scalar(scores[c][:, lo:hi], acc[:], SCORE_SCALE, None, ALU.mult)
                else:
                    nc.scalar.activation(scores[c][:, lo:hi], acc[:], ACT.Copy, scale=SCORE_SCALE)

            members = keep.tile([P, W], F32, name=f"members{c}")
            border = VECTOR_ENTRIES if first_tile else 0
            for first in range(0, border, PIECE):
                end = min(first + PIECE, border)
                nc.vector.tensor_copy(members[:, first:end], scores[c][:].indirect(entries(n3_sb, first, end)))
            cuts = list(range(border, W, PIECE)) + ([W - PIECE // 4] if last_tile else []) + [W]
            for first, end in zip(cuts, cuts[1:]):
                nc.scalar.activation(members[:, first:end], scores[c][:].indirect(entries(n3_sb, first, end)), ACT.Copy)

            if first_tile:
                stretch_ends = [U]
            elif last_tile:
                stretch_ends = [end // MEMBERS for end in cuts[1:]]
            else:
                stretch_ends = [BANK, U]
            groups = members[:].rearrange("p (w m) -> p w m", m=MEMBERS)
            high = ring.tile([P, 2 * U], F32, name="high")
            low = ring.tile([P, 2 * U], F32, name="low")
            high_pairs = high[:].rearrange("p (w m) -> p w m", m=2)
            low_pairs = low[:].rearrange("p (w m) -> p w m", m=2)
            for lo, hi in zip([0] + stretch_ends, stretch_ends):
                nc.vector.tensor_tensor(high_pairs[:, lo:hi, :], groups[:, lo:hi, 0:2], groups[:, lo:hi, 2:4], ALU.max)
                nc.vector.tensor_tensor(low_pairs[:, lo:hi, :], groups[:, lo:hi, 0:2], groups[:, lo:hi, 2:4], ALU.min)
                slots = slice(lo, hi)
                width = hi - lo
                largest = ring.tile([P, width], F32, name="largest")
                smallest = ring.tile([P, width], F32, name="smallest")
                nc.vector.tensor_tensor(largest[:], high_pairs[:, slots, 0], high_pairs[:, slots, 1], ALU.max)
                nc.vector.tensor_tensor(smallest[:], low_pairs[:, slots, 0], low_pairs[:, slots, 1], ALU.min)
                result = ring.tile([P, width], F32, name="result", bufs=3)
                nc.vector.scalar_tensor_tensor(result[:], smallest[:], -0.5, largest[:], ALU.mult, ALU.add)
                nc.sync.dma_start(out[cands, slots], result[:])
